import numpy as np
import ml_dtypes


def mxq(x, axis, fmt="e4m3"):
    dtype, down = {"e4m3": (ml_dtypes.float8_e4m3fn, 7), "e5m2": (ml_dtypes.float8_e5m2, 14)}[fmt]
    v = np.moveaxis(np.asarray(x, np.float32).astype(ml_dtypes.bfloat16).astype(np.float64), axis, -1)
    blocks = v.reshape(v.shape[:-1] + (-1, 32))
    amax = np.abs(blocks).max(-1, keepdims=True)
    byte = np.maximum(np.where(amax > 0, np.frexp(amax)[1] - 1 + 127, 0) - down, 1)
    scale = np.exp2(byte - 127.0)
    codes = (blocks / scale).astype(np.float32).astype(dtype).astype(np.float64)
    return np.moveaxis((codes * scale).reshape(v.shape), -1, axis)


WIDE = False


def mx_kscale(k):
    if not WIDE:
        return np.ones(k)
    levels = np.array([10, -10, 5, -5, 0])
    if k % 512:
        return np.exp2(np.random.permutation(np.resize(levels, k // 32))).repeat(32)
    a = np.empty((k // 512, 16))
    for p in range(k // 512):
        a[p, :8] = np.random.permutation(np.resize(levels, 8))
        for g in range(8):
            far = levels[np.abs(levels - a[p, g]) >= 10]
            a[p, g + 8] = far[np.random.randint(len(far))]
    return np.exp2(a.ravel()).repeat(32)


def f64(x):
    return np.asarray(x).astype(np.float64)


def striped(idx):
    return np.tile(idx.reshape(-1, 16).T, (8, 1)).astype(np.uint16)


def unstriped(offs):
    return offs[:16].T.reshape(-1).astype(np.int64)


E2M1 = np.array([0.0, 0.5, 1.0, 1.5, 2.0, 3.0, 4.0, 6.0, -0.0, -0.5, -1.0, -1.5, -2.0, -3.0, -4.0, -6.0])


def pack_weight(w, fmt):
    k, n = w.shape
    w = f64(np.asarray(w, np.float32).astype(ml_dtypes.bfloat16)).reshape(k // 32, 32, n)
    amax = np.abs(w).max(1)
    if fmt == "e4m3":
        byte = np.frexp(amax)[1] - 1 + 127 - 7
    else:
        mant, ex = np.frexp(amax / 6.0)
        byte = np.where(mant > 0.5, ex, ex - 1) + 127
    byte = np.clip(np.where(amax > 0, byte, 1), 1, 254)
    scaled = (w * np.exp2(127.0 - byte)[:, None, :]).reshape(k, n).astype(np.float32)
    by_word = np.ascontiguousarray(scaled.reshape(k // 512, 128, 4, n).transpose(0, 1, 3, 2))
    if fmt == "e4m3":
        words = by_word.astype(ml_dtypes.float8_e4m3fn).view(np.uint8)
    else:
        c = by_word.astype(ml_dtypes.float4_e2m1fn).view(np.uint8) & 0xF
        words = (c[..., 0::2] | (c[..., 1::2] << 4)).reshape(k // 512, 128, 2 * n)
    return np.ascontiguousarray(words), np.ascontiguousarray(byte.astype(np.uint8).reshape(k // 512, 16, n))


def unpack_weight(words, scales, fmt):
    g, _, n = scales.shape
    words = np.ascontiguousarray(words).reshape(g, 128, n, -1)
    if fmt == "e4m3":
        vals = words.view(ml_dtypes.float8_e4m3fn).astype(np.float64)
    else:
        nib = np.empty((g, 128, n, 4), np.uint8)
        nib[..., 0::2] = words & 0xF
        nib[..., 1::2] = words >> 4
        vals = E2M1[nib]
    vals = vals * np.repeat(np.exp2(scales.astype(np.float64) - 127.0), 8, axis=1)[..., None]
    return vals.transpose(0, 1, 3, 2).reshape(g * 512, n)


def gelu(v):
    return 0.5 * v * (1.0 + np.tanh(np.sqrt(2.0 / np.pi) * (v + 0.044715 * v**3)))


K, H, T, S, T3, S2, P = 1536, 512, 4096, 1024, 2048, 1024, 512

def setup_inputs():
    n = np.random.standard_normal
    s = mx_kscale(K)[:, None]
    u = mx_kscale(H)[:, None]
    d = {}
    d["tab_words"], d["tab_scales"] = pack_weight(n((K, T)) * s, "e4m3")
    d["offs"] = striped(np.random.permutation(T)[:S])
    d["tab2_words"], d["tab2_scales"] = pack_weight(n((H, T3)) / u / H ** 0.5, "e4m3")
    d["offs2"] = striped(np.random.permutation(T3)[:S2])
    d["pos1"] = striped(np.random.permutation(S)[:P])
    d["pos2"] = striped(np.random.permutation(S)[:P])
    d["w1"] = (2.0 * n((K, H)) / s / K ** 0.5).astype(np.float32)
    d["w4_words"], d["w4_scales"] = pack_weight(0.7 * n((K, H)) / s / K ** 0.5, "e2m1")
    d["gain"] = (np.exp(0.3 * n(H)) * u[:, 0]).astype(np.float32)
    d["wm"] = np.exp(0.4 * n(S2)).astype(np.float32)
    return d

def reference(tab_words, tab_scales, offs, tab2_words, tab2_scales, offs2, pos1, pos2,
              w1, w4_words, w4_scales, gain, wm):
    v = unpack_weight(tab_words, tab_scales, "e4m3")[:, unstriped(offs)]
    v2 = unpack_weight(tab2_words, tab2_scales, "e4m3")[:, unstriped(offs2)]
    w4 = unpack_weight(w4_words, w4_scales, "e2m1")
    ring = mxq(f64(w1), 0, "e4m3").T @ v
    trend = w4.T @ v
    h = f64(gain)[:, None] * (np.log(1.0 + np.abs(ring)) - trend)
    e = v2.T @ mxq(h, 0, "e4m3")
    core = e[:, unstriped(pos1)]
    margin = e[:, unstriped(pos2)]
    f = core + f64(wm)[:, None] * margin
    return f / (1.0 + np.exp(-f))

@@ -1,0 +1,336 @@
+from contextlib import ExitStack
+
+import concourse.mybir as mybir
+from concourse.masks import make_identity
+
+K, H, T, S, T3, S2, PAIRS = 1536, 512, 4096, 1024, 2048, 1024, 512
+FLOPS = 2 * K * H * S * 2 + 2 * H * S2 * S
+
+F32 = mybir.dt.float32
+BF16 = mybir.dt.bfloat16
+I32 = mybir.dt.int32
+U32 = mybir.dt.uint32
+U16 = mybir.dt.uint16
+U8 = mybir.dt.uint8
+FP8X4 = mybir.dt.float8_e4m3fn_x4
+FP4X4 = mybir.dt.float4_e2m1fn_x4
+ACT = mybir.ActivationFunctionType
+ALU = mybir.AluOpType
+
+P = 128
+PACK = 4
+K_PASS = P * PACK
+PASSES = K // K_PASS
+BANK = 512
+JT = S // P
+MT = S2 // P
+LANES = 16
+TAB2_ROW = 12
+PLANE_ROWS = 100
+
+
+def tile_list_otolith_stock_scores_kernel(
+    tc, tab_words, tab_scales, offs, tab2_words, tab2_scales, offs2, pos1, pos2,
+    w1, w4_words, w4_scales, gain, wm, out,
+):
+    nc = tc.nc
+    with ExitStack() as ctx:
+        keep = ctx.enter_context(tc.tile_pool(name="keep", bufs=1))
+        work = ctx.enter_context(tc.tile_pool(name="work", bufs=3))
+        psum = ctx.enter_context(tc.psum_pool(name="psum", bufs=1))
+
+        def bank(i):
+            return psum.tile([P, BANK], F32, name="bank%d" % i, tag="bank%d" % i)
+
+        def held(shape, dtype, name):
+            return keep.tile(shape, dtype, name=name, tag=name, align_bytes=64)
+
+        offs_sb = held([P, S // LANES], U16, "offs_sb")
+        offs2_sb = held([P, S2 // LANES], U16, "offs2_sb")
+        pos1_sb = held([P, PAIRS // LANES], U16, "pos1_sb")
+        pos2_sb = held([P, PAIRS // LANES], U16, "pos2_sb")
+        tab_sb = [held([P, T], I32, "tab_sb%d" % a) for a in range(PASSES)]
+        tab2_sb = held([P, T3], I32, "tab2_sb")
+        tabsc_sb = held([P, T], U8, "tabsc_sb")
+        tab2sc_sb = held([P, T3], U8, "tab2sc_sb")
+        w4_sb = held([P, PASSES, 2 * H], U8, "w4_sb")
+        w4sc_sb = held([P, PASSES, H], U8, "w4sc_sb")
+        shifted = [held([P, S], U8, "shifted%d" % a) for a in range(1, PASSES)]
+        wm_rows = held([P, P], F32, "wm_rows")
+        ident = held([P, P], F32, "ident")
+        gain_sb = held([P, PACK], F32, "gain_sb")
+        wm_sb = held([P, MT], F32, "wm_sb")
+
+        nc.vector.memset(tabsc_sb[:].bitcast(I32), 0)
+        nc.vector.memset(w4sc_sb[:].rearrange("p a c -> p (a c)").bitcast(I32), 0)
+        nc.vector.memset(tab2sc_sb[:].bitcast(I32), 0)
+        for plane in shifted:
+            nc.vector.memset(plane[:].bitcast(I32), 0)
+
+        for q in range(4):
+            nc.scalar.dma_start(
+                out=tabsc_sb[32 * q : 32 * q + 4 * PASSES, :].bitcast(I32),
+                in_=tab_scales[:, 4 * q : 4 * q + 4, :].bitcast(I32),
+            )
+        for q in range(4):
+            nc.gpsimd.dma_start(
+                out=w4sc_sb[32 * q : 32 * q + 4, :, :].bitcast(I32),
+                in_=w4_scales[:, 4 * q : 4 * q + 4, :].rearrange("a r c -> r a c").bitcast(I32),
+            )
+        for q in range(4):
+            nc.scalar.dma_start(
+                out=tab2sc_sb[32 * q + TAB2_ROW : 32 * q + TAB2_ROW + 4, :].bitcast(I32),
+                in_=tab2_scales[0, 4 * q : 4 * q + 4, :].bitcast(I32),
+            )
+        nc.gpsimd.dma_start(out=gain_sb[:], in_=gain.rearrange("(p t) -> p t", t=PACK))
+        make_identity(nc, ident[:])
+        nc.gpsimd.memset(wm_rows[:], 0.0)
+        nc.gpsimd.dma_start(out=wm_rows[0:MT, :], in_=wm.rearrange("(i p) -> i p", p=P))
+
+        def load_words(tile, words):
+            nc.sync.dma_start(out=tile[:], in_=words.rearrange("p t i -> p (t i)").bitcast(I32))
+
+        pieces = [(0, 0, H), (1, 0, H), (2, 0, H // 2), (2, H // 2, H)]
+        w1_raw = [held([P, PACK, c1 - c0], F32, "w1_raw%d" % i) for i, (a, c0, c1) in enumerate(pieces)]
+
+        nc.sync.dma_start(offs_sb[:], offs)
+        nc.sync.dma_start(offs2_sb[:], offs2)
+        load_words(tab_sb[0], tab_words[0])
+        load_words(tab_sb[1], tab_words[1])
+        nc.sync.dma_start(
+            out=w4_sb[:].bitcast(I32), in_=w4_words.rearrange("a p c -> p a c").bitcast(I32)
+        )
+        load_words(tab_sb[2], tab_words[2])
+        for raw, (a, c0, c1) in zip(w1_raw, pieces):
+            rows = w1[a * K_PASS : (a + 1) * K_PASS, c0:c1]
+            nc.sync.dma_start(out=raw[:], in_=rows.rearrange("(p i) c -> p i c", i=PACK))
+        load_words(tab2_sb, tab2_words[0])
+        nc.sync.dma_start(pos2_sb[:], pos2)
+        nc.sync.dma_start(pos1_sb[:], pos1)
+
+        v_sc = held([P, S], U8, "v_sc")
+        nc.vector.tensor_copy(out=v_sc[:], in_=tabsc_sb[:].indirect(offs_sb[:]))
+        for a in range(1, PASSES):
+            nc.scalar.dma_start(
+                out=shifted[a - 1][0:PLANE_ROWS, :].bitcast(I32),
+                in_=v_sc[4 * a : 4 * a + PLANE_ROWS, :].bitcast(I32),
+            )
+        v_planes = [v_sc] + shifted
+
+        def gather_words(dst, table, offsets, j0, j1):
+            nc.vector.tensor_copy(
+                out=dst[:, j0:j1],
+                in_=table[:].bitcast(U32).indirect(offsets[:, j0 // LANES : j1 // LANES]),
+            )
+
+        v_words = [held([P, S], U32, "v_words%d" % a) for a in range(PASSES)]
+
+        def jcols(jt):
+            return slice(jt * P, (jt + 1) * P)
+
+        def trend_pass(acc, jt, a):
+            nc.tensor.matmul_mx(
+                out=acc[:],
+                lhsT=v_words[a][:, jcols(jt)].bitcast(FP8X4),
+                lhsT_scale=v_planes[a][:, jcols(jt)],
+                rhs=w4_sb[:, a, :].bitcast(FP4X4),
+                rhs_scale=w4sc_sb[:, a, :],
+                start=(a == 0),
+                stop=(a == PASSES - 1),
+            )
+
+        trend_ps = [bank(jt) for jt in range(JT)]
+        for a in range(PASSES - 1):
+            gather_words(v_words[a], tab_sb[a], offs_sb, 0, S)
+            for jt in range(JT):
+                trend_pass(trend_ps[jt], jt, a)
+
+        v2_sc = held([P, S2], U8, "v2_sc")
+        nc.vector.tensor_copy(out=v2_sc[:], in_=tab2sc_sb[:].indirect(offs2_sb[:]))
+
+        neg_trend = [held([P, PACK, P], F32, "neg_trend%d" % jt) for jt in range(JT)]
+        for jt in range(JT):
+            if jt % 2 == 0:
+                gather_words(v_words[2], tab_sb[2], offs_sb, jt * P, (jt + 2) * P)
+            trend_pass(trend_ps[jt], jt, 2)
+            nc.scalar.activation(
+                out=neg_trend[jt][:],
+                in_=trend_ps[jt][:].rearrange("p (q t) -> p t q", t=PACK),
+                func=ACT.Copy,
+                scale=-1.0,
+            )
+
+        w1_bf = held([P, PASSES * H * PACK], BF16, "w1_bf")
+        w1_q = held([P, PASSES * H], U32, "w1_q")
+        w1_sc = held([P, PASSES * H], U8, "w1_sc")
+
+        def w1_round(i):
+            a, c0, c1 = pieces[i]
+            dst = w1_bf[:, (a * H + c0) * PACK : (a * H + c1) * PACK]
+            dst = dst.rearrange("p (c n i) -> p c i n", n=4, i=PACK)
+            src = w1_raw[i][:].rearrange("p i (c n) -> p c i n", n=4)
+            if i == 2:
+                nc.scalar.copy(out=dst, in_=src)
+            else:
+                nc.vector.tensor_copy(out=dst, in_=src)
+
+        def w1_quantise(i):
+            a, c0, c1 = pieces[i]
+            cols = slice(a * H + c0, a * H + c1)
+            nc.vector.quantize_mx(
+                out=w1_q[:, cols].bitcast(FP8X4),
+                scales=w1_sc[:, cols],
+                in_=w1_bf[:, (a * H + c0) * PACK : (a * H + c1) * PACK],
+            )
+
+        def ring_pass(acc, jt, a):
+            cols = slice(a * H, (a + 1) * H)
+            nc.tensor.matmul_mx(
+                out=acc[:],
+                lhsT=v_words[a][:, jcols(jt)].bitcast(FP8X4),
+                lhsT_scale=v_planes[a][:, jcols(jt)],
+                rhs=w1_q[:, cols].bitcast(FP8X4),
+                rhs_scale=w1_sc[:, cols],
+                start=(a == 0),
+                stop=(a == PASSES - 1),
+            )
+
+        early = JT - 2
+        ring_ps = [bank(jt) for jt in range(early)]
+        for a in range(PASSES - 1):
+            w1_round(a)
+            w1_quantise(a)
+            for jt in range(early):
+                ring_pass(ring_ps[jt], jt, a)
+        w1_round(2)
+        w1_round(3)
+        w1_quantise(2)
+        w1_quantise(3)
+
+        def add_transposed(acc, src, first):
+            for t in range(PACK):
+                nc.tensor.matmul(
+                    acc[:, t * P : (t + 1) * P],
+                    lhsT=src[:, t, :],
+                    rhs=ident[:],
+                    is_transpose=True,
+                    start=(first and t == 0),
+                    stop=(not first and t == PACK - 1),
+                )
+
+        diff_ps = {}
+        for jt in range(2):
+            diff_ps[jt] = bank(early + jt)
+            add_transposed(diff_ps[jt], neg_trend[jt], True)
+        for jt in range(early):
+            ring_pass(ring_ps[jt], jt, 2)
+
+        h_bf = held([P, S * PACK], BF16, "h_bf")
+        h_q = held([P, S], U32, "h_q")
+        h_sc = held([P, S], U8, "h_sc")
+        v2_words = held([P, S2], U32, "v2_words")
+        quantise_after = {3: 0, 6: 4, 7: 7}
+
+        for jt in range(JT):
+            mag = work.tile([P, PACK, P], F32, name="mag")
+            nc.scalar.activation(
+                out=mag[:], in_=ring_ps[jt][:].rearrange("p (q t) -> p t q", t=PACK), func=ACT.Abs
+            )
+            if jt < 2:
+                ring_ps.append(bank(jt))
+                for a in range(PASSES):
+                    ring_pass(ring_ps[early + jt], early + jt, a)
+            else:
+                diff_ps[jt] = bank(jt % early)
+                add_transposed(diff_ps[jt], neg_trend[jt], True)
+            logs = work.tile([P, PACK, P], F32, name="logs")
+            nc.scalar.activation(out=logs[:], in_=mag[:], func=ACT.Ln, bias=1.0)
+            add_transposed(diff_ps[jt], logs, False)
+            if jt < 4:
+                gather_words(v2_words, tab2_sb, offs2_sb, 2 * jt * P, 2 * (jt + 1) * P)
+            nc.vector.tensor_tensor(
+                out=h_bf[:, jt * K_PASS : (jt + 1) * K_PASS].rearrange("p (n t) -> p n t", t=PACK),
+                in0=diff_ps[jt][:].rearrange("p (t n) -> p n t", t=PACK),
+                in1=gain_sb[:].unsqueeze(1).to_broadcast([P, P, PACK]),
+                op=ALU.mult,
+            )
+            if jt in quantise_after:
+                j0, j1 = quantise_after[jt] * P, (jt + 1) * P
+                nc.vector.quantize_mx(
+                    out=h_q[:, j0:j1].bitcast(FP8X4),
+                    scales=h_sc[:, j0:j1],
+                    in_=h_bf[:, j0 * PACK : j1 * PACK],
+                )
+
+        wm_ps = bank(6)
+        nc.tensor.transpose(wm_ps[:, 0:P], wm_rows[:], ident[:])
+        nc.vector.tensor_copy(out=wm_sb[:], in_=wm_ps[:, 0:MT])
+
+        score_banks = [(6, 7), (2, 3), (4, 5), (0, 1)]
+        margins = {}
+        weighted = {}
+        sums = {}
+        scores = {}
+
+        def score_pass(acc, m, base, c0, c1):
+            nc.tensor.matmul_mx(
+                out=acc[:, c0:c1],
+                lhsT=v2_words[:, jcols(m)].bitcast(FP8X4),
+                lhsT_scale=v2_sc[TAB2_ROW:P, jcols(m)],
+                rhs=h_q[:, base + c0 : base + c1].bitcast(FP8X4),
+                rhs_scale=h_sc[:, base + c0 : base + c1],
+                start=True,
+                stop=True,
+            )
+
+        def make_scores(m):
+            scores[m] = work.tile([P, S], F32, name="scores", bufs=4)
+            for half in range(2):
+                cols = slice(half * BANK, (half + 1) * BANK)
+                acc = bank(score_banks[m % 4][half])
+                if m == 0 and half == 1:
+                    score_pass(acc, m, BANK, 0, 2 * P)
+                    score_pass(acc, m, BANK, 2 * P, 3 * P)
+                    nc.vector.tensor_copy(out=scores[m][:, BANK : BANK + 3 * P], in_=acc[:, 0 : 3 * P])
+                    score_pass(acc, m, BANK, 3 * P, BANK)
+                    nc.vector.tensor_copy(out=scores[m][:, BANK + 3 * P : S], in_=acc[:, 3 * P : BANK])
+                else:
+                    score_pass(acc, m, half * BANK, 0, BANK)
+                    nc.scalar.copy(out=scores[m][:, cols], in_=acc[:])
+            margins[m] = work.tile([P, PAIRS], F32, name="margin")
+            nc.vector.tensor_copy(out=margins[m][:], in_=scores[m][:].indirect(pos2_sb[:]))
+
+        def weigh(m):
+            weighted[m] = work.tile([P, PAIRS], F32, name="weighted")
+            nc.scalar.activation(
+                out=weighted[m][:], in_=margins[m][:], func=ACT.Copy, scale=wm_sb[:, m : m + 1]
+            )
+
+        def parts(m):
+            n = 2 if m == MT - 1 else 1
+            return [(i * PAIRS // n, (i + 1) * PAIRS // n) for i in range(n)]
+
+        def add_cores(m):
+            sums[m] = work.tile([P, PAIRS], F32, name="sums")
+            for c0, c1 in parts(m):
+                nc.vector.tensor_tensor(
+                    out=sums[m][:, c0:c1],
+                    in0=scores[m][:].indirect(pos1_sb[:, c0 // LANES : c1 // LANES]),
+                    in1=weighted[m][:, c0:c1],
+                    op=ALU.add,
+                )
+
+        def finish(m):
+            result = work.tile([P, PAIRS], F32, name="result")
+            for c0, c1 in parts(m):
+                nc.scalar.activation(out=result[:, c0:c1], in_=sums[m][:, c0:c1], func=ACT.Silu)
+                nc.sync.dma_start(out=out[m * P : (m + 1) * P, c0:c1], in_=result[:, c0:c1])
+
+        for step in range(MT + 2):
+            if step < MT:
+                make_scores(step)
+            if 1 <= step <= MT:
+                weigh(step - 1)
+                add_cores(step - 1)
+            if step >= 2:
+                finish(step - 2)

@@ -26,7 +26,7 @@ JT = S // P
 MT = S2 // P
 LANES = 16
 TAB2_ROW = 12
-PLANE_ROWS = 100
+HALF = H // 2
 
 
 def tile_list_otolith_stock_scores_kernel(
@@ -55,67 +55,80 @@ def tile_list_otolith_stock_scores_kernel(
         tab2sc_sb = held([P, T3], U8, "tab2sc_sb")
         w4_sb = held([P, PASSES, 2 * H], U8, "w4_sb")
         w4sc_sb = held([P, PASSES, H], U8, "w4sc_sb")
-        shifted = [held([P, S], U8, "shifted%d" % a) for a in range(1, PASSES)]
+        v_planes = held([P, PASSES, S], U8, "v_planes")
         wm_rows = held([P, P], F32, "wm_rows")
         ident = held([P, P], F32, "ident")
         gain_sb = held([P, PACK], F32, "gain_sb")
-        wm_sb = held([P, MT], F32, "wm_sb")
 
         nc.vector.memset(tabsc_sb[:].bitcast(I32), 0)
         nc.vector.memset(w4sc_sb[:].rearrange("p a c -> p (a c)").bitcast(I32), 0)
         nc.vector.memset(tab2sc_sb[:].bitcast(I32), 0)
-        for plane in shifted:
-            nc.vector.memset(plane[:].bitcast(I32), 0)
+        nc.vector.memset(v_planes[:].rearrange("p a j -> p (a j)").bitcast(I32), 0)
 
-        for q in range(4):
-            nc.scalar.dma_start(
-                out=tabsc_sb[32 * q : 32 * q + 4 * PASSES, :].bitcast(I32),
-                in_=tab_scales[:, 4 * q : 4 * q + 4, :].bitcast(I32),
-            )
+        nc.gpsimd.memset(wm_rows[:], 0.0)
+        nc.gpsimd.dma_start(out=wm_rows[0:MT, :], in_=wm.rearrange("(i p) -> i p", p=P))
+        make_identity(nc, ident[:])
         for q in range(4):
             nc.gpsimd.dma_start(
                 out=w4sc_sb[32 * q : 32 * q + 4, :, :].bitcast(I32),
                 in_=w4_scales[:, 4 * q : 4 * q + 4, :].rearrange("a r c -> r a c").bitcast(I32),
             )
-        for q in range(4):
-            nc.scalar.dma_start(
-                out=tab2sc_sb[32 * q + TAB2_ROW : 32 * q + TAB2_ROW + 4, :].bitcast(I32),
-                in_=tab2_scales[0, 4 * q : 4 * q + 4, :].bitcast(I32),
-            )
         nc.gpsimd.dma_start(out=gain_sb[:], in_=gain.rearrange("(p t) -> p t", t=PACK))
-        make_identity(nc, ident[:])
-        nc.gpsimd.memset(wm_rows[:], 0.0)
-        nc.gpsimd.dma_start(out=wm_rows[0:MT, :], in_=wm.rearrange("(i p) -> i p", p=P))
 
-        def load_words(tile, words):
-            nc.sync.dma_start(out=tile[:], in_=words.rearrange("p t i -> p (t i)").bitcast(I32))
+        def load_words(tile, words, t0, t1):
+            nc.sync.dma_start(
+                out=tile[:, t0:t1], in_=words[:, t0:t1, :].rearrange("p t i -> p (t i)").bitcast(I32)
+            )
 
-        pieces = [(0, 0, H), (1, 0, H), (2, 0, H // 2), (2, H // 2, H)]
-        w1_raw = [held([P, PACK, c1 - c0], F32, "w1_raw%d" % i) for i, (a, c0, c1) in enumerate(pieces)]
+        pieces = [(half, a) for half in range(2) for a in range(PASSES)]
+        w1_raw = held([P, len(pieces), PACK, HALF], F32, "w1_raw")
 
         nc.sync.dma_start(offs_sb[:], offs)
-        nc.sync.dma_start(offs2_sb[:], offs2)
-        load_words(tab_sb[0], tab_words[0])
-        load_words(tab_sb[1], tab_words[1])
+        load_words(tab_sb[0], tab_words[0], 0, T // 2)
+        for a in range(PASSES):
+            nc.sync.dma_start(
+                out=tabsc_sb[32 * a + 16 : 32 * a + 32, :].bitcast(I32), in_=tab_scales[a].bitcast(I32)
+            )
+        load_words(tab_sb[0], tab_words[0], T // 2, T)
         nc.sync.dma_start(
             out=w4_sb[:].bitcast(I32), in_=w4_words.rearrange("a p c -> p a c").bitcast(I32)
         )
-        load_words(tab_sb[2], tab_words[2])
-        for raw, (a, c0, c1) in zip(w1_raw, pieces):
-            rows = w1[a * K_PASS : (a + 1) * K_PASS, c0:c1]
-            nc.sync.dma_start(out=raw[:], in_=rows.rearrange("(p i) c -> p i c", i=PACK))
-        load_words(tab2_sb, tab2_words[0])
-        nc.sync.dma_start(pos2_sb[:], pos2)
-        nc.sync.dma_start(pos1_sb[:], pos1)
+        nc.sync.dma_start(offs2_sb[:], offs2)
+        for q in range(4):
+            nc.sync.dma_start(
+                out=tab2sc_sb[32 * q + TAB2_ROW : 32 * q + TAB2_ROW + 4, :].bitcast(I32),
+                in_=tab2_scales[0, 4 * q : 4 * q + 4, :].bitcast(I32),
+            )
+
+        wm_ps = bank(7)
+        nc.tensor.transpose(wm_ps[:, 0:P], wm_rows[:], ident[:])
+        wm_wide = [held([P, PAIRS], F32, "pairs%d" % m) for m in range(MT)]
+        for m in range(MT):
+            nc.scalar.copy(out=wm_wide[m][:], in_=wm_ps[:, m : m + 1].to_broadcast([P, PAIRS]))
 
         v_sc = held([P, S], U8, "v_sc")
         nc.vector.tensor_copy(out=v_sc[:], in_=tabsc_sb[:].indirect(offs_sb[:]))
-        for a in range(1, PASSES):
-            nc.scalar.dma_start(
-                out=shifted[a - 1][0:PLANE_ROWS, :].bitcast(I32),
-                in_=v_sc[4 * a : 4 * a + PLANE_ROWS, :].bitcast(I32),
-            )
-        v_planes = [v_sc] + shifted
+
+        def place_scale_rows(a):
+            for q in range(4):
+                row = 32 * a + 16 + 4 * q
+                nc.sync.dma_start(
+                    out=v_planes[32 * q : 32 * q + 4, a, :].bitcast(I32),
+                    in_=v_sc[row : row + 4, :].bitcast(I32),
+                )
+
+        load_words(tab_sb[1], tab_words[1], 0, T // 2)
+        place_scale_rows(0)
+        load_words(tab_sb[1], tab_words[1], T // 2, T)
+        place_scale_rows(1)
+        load_words(tab_sb[2], tab_words[2], 0, T)
+        place_scale_rows(2)
+        for i, (half, a) in enumerate(pieces):
+            rows = w1[a * K_PASS : (a + 1) * K_PASS, half * HALF : (half + 1) * HALF]
+            nc.sync.dma_start(out=w1_raw[:, i], in_=rows.rearrange("(p i) c -> p i c", i=PACK))
+        load_words(tab2_sb, tab2_words[0], 0, T3)
+        nc.sync.dma_start(pos2_sb[:], pos2)
+        nc.sync.dma_start(pos1_sb[:], pos1)
 
         def gather_words(dst, table, offsets, j0, j1):
             nc.vector.tensor_copy(
@@ -132,7 +145,7 @@ def tile_list_otolith_stock_scores_kernel(
             nc.tensor.matmul_mx(
                 out=acc[:],
                 lhsT=v_words[a][:, jcols(jt)].bitcast(FP8X4),
-                lhsT_scale=v_planes[a][:, jcols(jt)],
+                lhsT_scale=v_planes[:, a, jcols(jt)],
                 rhs=w4_sb[:, a, :].bitcast(FP4X4),
                 rhs_scale=w4sc_sb[:, a, :],
                 start=(a == 0),
@@ -141,8 +154,9 @@ def tile_list_otolith_stock_scores_kernel(
 
         trend_ps = [bank(jt) for jt in range(JT)]
         for a in range(PASSES - 1):
-            gather_words(v_words[a], tab_sb[a], offs_sb, 0, S)
             for jt in range(JT):
+                if jt % 2 == 0:
+                    gather_words(v_words[a], tab_sb[a], offs_sb, jt * P, (jt + 2) * P)
                 trend_pass(trend_ps[jt], jt, a)
 
         v2_sc = held([P, S2], U8, "v2_sc")
@@ -164,48 +178,32 @@ def tile_list_otolith_stock_scores_kernel(
         w1_q = held([P, PASSES * H], U32, "w1_q")
         w1_sc = held([P, PASSES * H], U8, "w1_sc")
 
-        def w1_round(i):
-            a, c0, c1 = pieces[i]
-            dst = w1_bf[:, (a * H + c0) * PACK : (a * H + c1) * PACK]
-            dst = dst.rearrange("p (c n i) -> p c i n", n=4, i=PACK)
-            src = w1_raw[i][:].rearrange("p i (c n) -> p c i n", n=4)
-            if i == 2:
-                nc.scalar.copy(out=dst, in_=src)
-            else:
-                nc.vector.tensor_copy(out=dst, in_=src)
-
-        def w1_quantise(i):
-            a, c0, c1 = pieces[i]
-            cols = slice(a * H + c0, a * H + c1)
-            nc.vector.quantize_mx(
-                out=w1_q[:, cols].bitcast(FP8X4),
-                scales=w1_sc[:, cols],
-                in_=w1_bf[:, (a * H + c0) * PACK : (a * H + c1) * PACK],
+        def w1_quantise(i0, i1):
+            cols = slice(i0 * HALF, i1 * HALF)
+            rounded = w1_bf[:, i0 * HALF * PACK : i1 * HALF * PACK]
+            nc.vector.tensor_copy(
+                out=rounded.rearrange("p (a c n i) -> p a c i n", a=i1 - i0, n=4, i=PACK),
+                in_=w1_raw[:, i0:i1].rearrange("p a i (c n) -> p a c i n", n=4),
             )
+            nc.vector.quantize_mx(out=w1_q[:, cols].bitcast(FP8X4), scales=w1_sc[:, cols], in_=rounded)
 
-        def ring_pass(acc, jt, a):
-            cols = slice(a * H, (a + 1) * H)
-            nc.tensor.matmul_mx(
-                out=acc[:],
-                lhsT=v_words[a][:, jcols(jt)].bitcast(FP8X4),
-                lhsT_scale=v_planes[a][:, jcols(jt)],
-                rhs=w1_q[:, cols].bitcast(FP8X4),
-                rhs_scale=w1_sc[:, cols],
-                start=(a == 0),
-                stop=(a == PASSES - 1),
-            )
-
-        early = JT - 2
-        ring_ps = [bank(jt) for jt in range(early)]
-        for a in range(PASSES - 1):
-            w1_round(a)
-            w1_quantise(a)
-            for jt in range(early):
-                ring_pass(ring_ps[jt], jt, a)
-        w1_round(2)
-        w1_round(3)
-        w1_quantise(2)
-        w1_quantise(3)
+        ring_ps = [[bank(half * 4 + pair) for pair in range(JT // 2)] for half in range(2)]
+        for i, (half, a) in enumerate(pieces):
+            if a == 0:
+                w1_quantise(i, i + 2)
+            if a == 2:
+                w1_quantise(i, i + 1)
+            cols = slice(i * HALF, (i + 1) * HALF)
+            for jt in range(JT):
+                nc.tensor.matmul_mx(
+                    out=ring_ps[half][jt // 2][:, (jt % 2) * HALF : (jt % 2 + 1) * HALF],
+                    lhsT=v_words[a][:, jcols(jt)].bitcast(FP8X4),
+                    lhsT_scale=v_planes[:, a, jcols(jt)],
+                    rhs=w1_q[:, cols].bitcast(FP8X4),
+                    rhs_scale=w1_sc[:, cols],
+                    start=(a == 0 and jt % 2 == 0),
+                    stop=(a == PASSES - 1 and jt % 2 == 1),
+                )
 
         def add_transposed(acc, src, first):
             for t in range(PACK):
@@ -218,38 +216,43 @@ def tile_list_otolith_stock_scores_kernel(
                     stop=(not first and t == PACK - 1),
                 )
 
-        diff_ps = {}
-        for jt in range(2):
-            diff_ps[jt] = bank(early + jt)
-            add_transposed(diff_ps[jt], neg_trend[jt], True)
-        for jt in range(early):
-            ring_pass(ring_ps[jt], jt, 2)
-
-        h_bf = held([P, S * PACK], BF16, "h_bf")
+        h_bf = held([P, (S - P) * PACK], BF16, "h_bf")
+        h_bf_last = held([P, P * PACK], BF16, "h_bf_last")
         h_q = held([P, S], U32, "h_q")
         h_sc = held([P, S], U8, "h_sc")
-        v2_words = held([P, S2], U32, "v2_words")
+        v2_words = []
+
+        def gather_stocks(i, name):
+            v2_words.append(held([P, 2 * P], U32, name))
+            nc.vector.tensor_copy(
+                out=v2_words[i][:],
+                in_=tab2_sb[:].bitcast(U32).indirect(offs2_sb[:, 2 * i * P // LANES : 2 * (i + 1) * P // LANES]),
+            )
+
+        logs = [held([P, 2, PACK, P], F32, "logs%d" % pair) for pair in range(JT // 2)]
         quantise_after = {3: 0, 6: 4, 7: 7}
 
-        for jt in range(JT):
-            mag = work.tile([P, PACK, P], F32, name="mag")
-            nc.scalar.activation(
-                out=mag[:], in_=ring_ps[jt][:].rearrange("p (q t) -> p t q", t=PACK), func=ACT.Abs
-            )
-            if jt < 2:
-                ring_ps.append(bank(jt))
-                for a in range(PASSES):
-                    ring_pass(ring_ps[early + jt], early + jt, a)
-            else:
-                diff_ps[jt] = bank(jt % early)
-                add_transposed(diff_ps[jt], neg_trend[jt], True)
-            logs = work.tile([P, PACK, P], F32, name="logs")
-            nc.scalar.activation(out=logs[:], in_=mag[:], func=ACT.Ln, bias=1.0)
-            add_transposed(diff_ps[jt], logs, False)
-            if jt < 4:
-                gather_words(v2_words, tab2_sb, offs2_sb, 2 * jt * P, 2 * (jt + 1) * P)
+        def magnitudes(half, pair, u0, u1):
+            mag = work.tile([P, u1 - u0, PACK, P // 2], F32, name="mag")
+            ring = ring_ps[half][pair][:].rearrange("p (u q t) -> p u t q", u=2, t=PACK)
+            nc.scalar.activation(out=mag[:], in_=ring[:, u0:u1], func=ACT.Abs)
+            return mag
+
+        def logarithms(half, pair, u0, u1, mag):
+            rows = slice(half * P // 2, (half + 1) * P // 2)
+            nc.scalar.activation(out=logs[pair][:, u0:u1, :, rows], in_=mag[:], func=ACT.Ln, bias=1.0)
+
+        diff_ps = {}
+
+        def open_difference(jt):
+            diff_ps[jt] = bank(jt)
+            add_transposed(diff_ps[jt], neg_trend[jt], True)
+
+        def finish_features(jt):
+            add_transposed(diff_ps[jt], logs[jt // 2][:, jt % 2], False)
+            rounded = h_bf_last[:] if jt == JT - 1 else h_bf[:, jt * K_PASS : (jt + 1) * K_PASS]
             nc.vector.tensor_tensor(
-                out=h_bf[:, jt * K_PASS : (jt + 1) * K_PASS].rearrange("p (n t) -> p n t", t=PACK),
+                out=rounded.rearrange("p (n t) -> p n t", t=PACK),
                 in0=diff_ps[jt][:].rearrange("p (t n) -> p n t", t=PACK),
                 in1=gain_sb[:].unsqueeze(1).to_broadcast([P, P, PACK]),
                 op=ALU.mult,
@@ -259,23 +262,40 @@ def tile_list_otolith_stock_scores_kernel(
                 nc.vector.quantize_mx(
                     out=h_q[:, j0:j1].bitcast(FP8X4),
                     scales=h_sc[:, j0:j1],
-                    in_=h_bf[:, j0 * PACK : j1 * PACK],
+                    in_=rounded if jt == JT - 1 else h_bf[:, j0 * PACK : j1 * PACK],
                 )
 
-        wm_ps = bank(6)
-        nc.tensor.transpose(wm_ps[:, 0:P], wm_rows[:], ident[:])
-        nc.vector.tensor_copy(out=wm_sb[:], in_=wm_ps[:, 0:MT])
+        for pair in range(JT // 2):
+            mag = magnitudes(0, pair, 0, 2)
+            open_difference(pair)
+            logarithms(0, pair, 0, 2, mag)
+        for i in range(3):
+            gather_stocks(i, "v2_words%d" % i)
+        last = JT // 2 - 1
+        for pair in range(last):
+            mag = magnitudes(1, pair, 0, 2)
+            logarithms(1, pair, 0, 2, mag)
+            finish_features(2 * pair)
+            open_difference(JT // 2 + pair)
+            finish_features(2 * pair + 1)
+        mag = magnitudes(1, last, 0, 1)
+        logarithms(1, last, 0, 1, mag)
+        mag = magnitudes(1, last, 1, 2)
+        open_difference(JT - 1)
+        finish_features(JT - 2)
+        logarithms(1, last, 1, 2, mag)
+        finish_features(JT - 1)
+        gather_stocks(3, "h_bf_last")
 
-        score_banks = [(6, 7), (2, 3), (4, 5), (0, 1)]
+        score_banks = [(0, 1), (2, 3), (4, 5), (6, 7)]
         margins = {}
-        weighted = {}
         sums = {}
         scores = {}
 
         def score_pass(acc, m, base, c0, c1):
             nc.tensor.matmul_mx(
                 out=acc[:, c0:c1],
-                lhsT=v2_words[:, jcols(m)].bitcast(FP8X4),
+                lhsT=v2_words[m // 2][:, jcols(m % 2)].bitcast(FP8X4),
                 lhsT_scale=v2_sc[TAB2_ROW:P, jcols(m)],
                 rhs=h_q[:, base + c0 : base + c1].bitcast(FP8X4),
                 rhs_scale=h_sc[:, base + c0 : base + c1],
@@ -291,32 +311,29 @@ def tile_list_otolith_stock_scores_kernel(
                 if m == 0 and half == 1:
                     score_pass(acc, m, BANK, 0, 2 * P)
                     score_pass(acc, m, BANK, 2 * P, 3 * P)
-                    nc.vector.tensor_copy(out=scores[m][:, BANK : BANK + 3 * P], in_=acc[:, 0 : 3 * P])
+                    nc.scalar.copy(out=scores[m][:, BANK : BANK + 3 * P], in_=acc[:, 0 : 3 * P])
                     score_pass(acc, m, BANK, 3 * P, BANK)
-                    nc.vector.tensor_copy(out=scores[m][:, BANK + 3 * P : S], in_=acc[:, 3 * P : BANK])
+                    nc.scalar.copy(out=scores[m][:, BANK + 3 * P : S], in_=acc[:, 3 * P : BANK])
                 else:
                     score_pass(acc, m, half * BANK, 0, BANK)
                     nc.scalar.copy(out=scores[m][:, cols], in_=acc[:])
             margins[m] = work.tile([P, PAIRS], F32, name="margin")
-            nc.vector.tensor_copy(out=margins[m][:], in_=scores[m][:].indirect(pos2_sb[:]))
-
-        def weigh(m):
-            weighted[m] = work.tile([P, PAIRS], F32, name="weighted")
-            nc.scalar.activation(
-                out=weighted[m][:], in_=margins[m][:], func=ACT.Copy, scale=wm_sb[:, m : m + 1]
+            nc.vector.tensor_tensor(
+                out=margins[m][:], in0=scores[m][:].indirect(pos2_sb[:]), in1=wm_wide[m][:], op=ALU.mult
             )
 
         def parts(m):
-            n = 2 if m == MT - 1 else 1
-            return [(i * PAIRS // n, (i + 1) * PAIRS // n) for i in range(n)]
+            if m < MT - 1:
+                return [(0, PAIRS)]
+            return [(0, 2 * P), (2 * P, 3 * P), (3 * P, PAIRS)]
 
         def add_cores(m):
-            sums[m] = work.tile([P, PAIRS], F32, name="sums")
+            sums[m] = work.tile([P, PAIRS], F32, name="sums", bufs=2)
             for c0, c1 in parts(m):
                 nc.vector.tensor_tensor(
                     out=sums[m][:, c0:c1],
                     in0=scores[m][:].indirect(pos1_sb[:, c0 // LANES : c1 // LANES]),
-                    in1=weighted[m][:, c0:c1],
+                    in1=margins[m][:, c0:c1],
                     op=ALU.add,
                 )
 
@@ -326,11 +343,10 @@ def tile_list_otolith_stock_scores_kernel(
                 nc.scalar.activation(out=result[:, c0:c1], in_=sums[m][:, c0:c1], func=ACT.Silu)
                 nc.sync.dma_start(out=out[m * P : (m + 1) * P, c0:c1], in_=result[:, c0:c1])
 
-        for step in range(MT + 2):
+        for step in range(MT + 3):
             if step < MT:
                 make_scores(step)
+            if step >= 3:
+                finish(step - 3)
             if 1 <= step <= MT:
-                weigh(step - 1)
                 add_cores(step - 1)
-            if step >= 2:
-                finish(step - 2)

@@ -68,10 +68,10 @@ def tile_list_otolith_stock_scores_kernel(
         nc.gpsimd.memset(wm_rows[:], 0.0)
         nc.gpsimd.dma_start(out=wm_rows[0:MT, :], in_=wm.rearrange("(i p) -> i p", p=P))
         make_identity(nc, ident[:])
-        for q in range(4):
+        for r in range(4):
             nc.gpsimd.dma_start(
-                out=w4sc_sb[32 * q : 32 * q + 4, :, :].bitcast(I32),
-                in_=w4_scales[:, 4 * q : 4 * q + 4, :].rearrange("a r c -> r a c").bitcast(I32),
+                out=w4sc_sb[r:P:32, :, :].bitcast(I32),
+                in_=w4_scales[:, r:16:4, :].rearrange("a q c -> q a c").bitcast(I32),
             )
         nc.gpsimd.dma_start(out=gain_sb[:], in_=gain.rearrange("(p t) -> p t", t=PACK))
 
@@ -85,44 +85,44 @@ def tile_list_otolith_stock_scores_kernel(
 
         nc.sync.dma_start(offs_sb[:], offs)
         load_words(tab_sb[0], tab_words[0], 0, T // 2)
-        for a in range(PASSES):
-            nc.sync.dma_start(
-                out=tabsc_sb[32 * a + 16 : 32 * a + 32, :].bitcast(I32), in_=tab_scales[a].bitcast(I32)
-            )
+        nc.sync.dma_start(
+            out=tabsc_sb[0:P:4, :].bitcast(I32),
+            in_=tab_scales[0:2].rearrange("a q t -> (a q) t").bitcast(I32),
+        )
+        nc.sync.dma_start(out=tabsc_sb[1:P:8, :].bitcast(I32), in_=tab_scales[2].bitcast(I32))
         load_words(tab_sb[0], tab_words[0], T // 2, T)
         nc.sync.dma_start(
             out=w4_sb[:].bitcast(I32), in_=w4_words.rearrange("a p c -> p a c").bitcast(I32)
         )
         nc.sync.dma_start(offs2_sb[:], offs2)
-        for q in range(4):
+        for r in range(4):
             nc.sync.dma_start(
-                out=tab2sc_sb[32 * q + TAB2_ROW : 32 * q + TAB2_ROW + 4, :].bitcast(I32),
-                in_=tab2_scales[0, 4 * q : 4 * q + 4, :].bitcast(I32),
+                out=tab2sc_sb[TAB2_ROW + r : P : 32, :].bitcast(I32),
+                in_=tab2_scales[0, r:16:4, :].bitcast(I32),
             )
 
         wm_ps = bank(7)
         nc.tensor.transpose(wm_ps[:, 0:P], wm_rows[:], ident[:])
-        wm_wide = [held([P, PAIRS], F32, "pairs%d" % m) for m in range(MT)]
-        for m in range(MT):
-            nc.scalar.copy(out=wm_wide[m][:], in_=wm_ps[:, m : m + 1].to_broadcast([P, PAIRS]))
+        wm_sb = held([P, MT], F32, "wm_sb")
+        nc.scalar.copy(out=wm_sb[:], in_=wm_ps[:, 0:MT])
 
         v_sc = held([P, S], U8, "v_sc")
         nc.vector.tensor_copy(out=v_sc[:], in_=tabsc_sb[:].indirect(offs_sb[:]))
 
         def place_scale_rows(a):
-            for q in range(4):
-                row = 32 * a + 16 + 4 * q
+            for r in range(4):
+                rows = slice(64 * a + 4 * r, 64 * a + 64, 16) if a < 2 else slice(8 * r + 1, P, 32)
                 nc.sync.dma_start(
-                    out=v_planes[32 * q : 32 * q + 4, a, :].bitcast(I32),
-                    in_=v_sc[row : row + 4, :].bitcast(I32),
+                    out=v_planes[r:P:32, a, :].bitcast(I32), in_=v_sc[rows, :].bitcast(I32)
                 )
 
         load_words(tab_sb[1], tab_words[1], 0, T // 2)
         place_scale_rows(0)
         load_words(tab_sb[1], tab_words[1], T // 2, T)
         place_scale_rows(1)
-        load_words(tab_sb[2], tab_words[2], 0, T)
+        load_words(tab_sb[2], tab_words[2], 0, T // 2)
         place_scale_rows(2)
+        load_words(tab_sb[2], tab_words[2], T // 2, T)
         for i, (half, a) in enumerate(pieces):
             rows = w1[a * K_PASS : (a + 1) * K_PASS, half * HALF : (half + 1) * HALF]
             nc.sync.dma_start(out=w1_raw[:, i], in_=rows.rearrange("(p i) c -> p i c", i=PACK))
@@ -289,6 +289,7 @@ def tile_list_otolith_stock_scores_kernel(
 
         score_banks = [(0, 1), (2, 3), (4, 5), (6, 7)]
         margins = {}
+        weighted = {}
         sums = {}
         scores = {}
 
@@ -318,8 +319,12 @@ def tile_list_otolith_stock_scores_kernel(
                     score_pass(acc, m, half * BANK, 0, BANK)
                     nc.scalar.copy(out=scores[m][:, cols], in_=acc[:])
             margins[m] = work.tile([P, PAIRS], F32, name="margin")
-            nc.vector.tensor_tensor(
-                out=margins[m][:], in0=scores[m][:].indirect(pos2_sb[:]), in1=wm_wide[m][:], op=ALU.mult
+            nc.vector.tensor_copy(out=margins[m][:], in_=scores[m][:].indirect(pos2_sb[:]))
+
+        def weigh(m):
+            weighted[m] = work.tile([P, PAIRS], F32, name="weighted")
+            nc.scalar.activation(
+                out=weighted[m][:], in_=margins[m][:], func=ACT.Copy, scale=wm_sb[:, m : m + 1]
             )
 
         def parts(m):
@@ -328,12 +333,12 @@ def tile_list_otolith_stock_scores_kernel(
             return [(0, 2 * P), (2 * P, 3 * P), (3 * P, PAIRS)]
 
         def add_cores(m):
-            sums[m] = work.tile([P, PAIRS], F32, name="sums", bufs=2)
+            sums[m] = work.tile([P, PAIRS], F32, name="sums", bufs=4)
             for c0, c1 in parts(m):
                 nc.vector.tensor_tensor(
                     out=sums[m][:, c0:c1],
                     in0=scores[m][:].indirect(pos1_sb[:, c0 // LANES : c1 // LANES]),
-                    in1=margins[m][:, c0:c1],
+                    in1=weighted[m][:, c0:c1],
                     op=ALU.add,
                 )
 
@@ -346,7 +351,8 @@ def tile_list_otolith_stock_scores_kernel(
         for step in range(MT + 3):
             if step < MT:
                 make_scores(step)
+            if 1 <= step <= MT:
+                weigh(step - 1)
+                add_cores(step - 1)
             if step >= 3:
                 finish(step - 3)
-            if 1 <= step <= MT:
-                add_cores(step - 1)

@@ -101,6 +101,9 @@ def tile_list_otolith_stock_scores_kernel(
                 in_=tab2_scales[0, r:16:4, :].bitcast(I32),
             )
 
+        warm = held([P, 1], F32, "warm")
+        nc.scalar.activation(out=warm[:], in_=ident[:, 0:1], func=ACT.Ln, bias=1.0)
+
         wm_ps = bank(7)
         nc.tensor.transpose(wm_ps[:, 0:P], wm_rows[:], ident[:])
         wm_sb = held([P, MT], F32, "wm_sb")

from contextlib import ExitStack

import concourse.mybir as mybir
from concourse.masks import make_identity

K, H, T, S, T3, S2, PAIRS = 1536, 512, 4096, 1024, 2048, 1024, 512
FLOPS = 2 * K * H * S * 2 + 2 * H * S2 * S

F32 = mybir.dt.float32
BF16 = mybir.dt.bfloat16
I32 = mybir.dt.int32
U32 = mybir.dt.uint32
U16 = mybir.dt.uint16
U8 = mybir.dt.uint8
FP8X4 = mybir.dt.float8_e4m3fn_x4
FP4X4 = mybir.dt.float4_e2m1fn_x4
ACT = mybir.ActivationFunctionType
ALU = mybir.AluOpType

P = 128
PACK = 4
K_PASS = P * PACK
PASSES = K // K_PASS
BANK = 512
JT = S // P
MT = S2 // P
LANES = 16
TAB2_ROW = 12
HALF = H // 2


def tile_list_otolith_stock_scores_kernel(
    tc, tab_words, tab_scales, offs, tab2_words, tab2_scales, offs2, pos1, pos2,
    w1, w4_words, w4_scales, gain, wm, out,
):
    nc = tc.nc
    with ExitStack() as ctx:
        keep = ctx.enter_context(tc.tile_pool(name="keep", bufs=1))
        work = ctx.enter_context(tc.tile_pool(name="work", bufs=3))
        psum = ctx.enter_context(tc.psum_pool(name="psum", bufs=1))

        def bank(i):
            return psum.tile([P, BANK], F32, name="bank%d" % i, tag="bank%d" % i)

        def held(shape, dtype, name):
            return keep.tile(shape, dtype, name=name, tag=name, align_bytes=64)

        offs_sb = held([P, S // LANES], U16, "offs_sb")
        offs2_sb = held([P, S2 // LANES], U16, "offs2_sb")
        pos1_sb = held([P, PAIRS // LANES], U16, "pos1_sb")
        pos2_sb = held([P, PAIRS // LANES], U16, "pos2_sb")
        tab_sb = [held([P, T], I32, "tab_sb%d" % a) for a in range(PASSES)]
        tab2_sb = held([P, T3], I32, "tab2_sb")
        tabsc_sb = held([P, T], U8, "tabsc_sb")
        tab2sc_sb = held([P, T3], U8, "tab2sc_sb")
        w4_sb = held([P, PASSES, 2 * H], U8, "w4_sb")
        w4sc_sb = held([P, PASSES, H], U8, "w4sc_sb")
        v_planes = held([P, PASSES, S], U8, "v_planes")
        wm_rows = held([P, P], F32, "wm_rows")
        ident = held([P, P], F32, "ident")
        gain_sb = held([P, PACK], F32, "gain_sb")

        nc.vector.memset(tabsc_sb[:].bitcast(I32), 0)
        nc.vector.memset(w4sc_sb[:].rearrange("p a c -> p (a c)").bitcast(I32), 0)
        nc.vector.memset(tab2sc_sb[:].bitcast(I32), 0)
        nc.vector.memset(v_planes[:].rearrange("p a j -> p (a j)").bitcast(I32), 0)

        nc.gpsimd.memset(wm_rows[:], 0.0)
        nc.gpsimd.dma_start(out=wm_rows[0:MT, :], in_=wm.rearrange("(i p) -> i p", p=P))
        make_identity(nc, ident[:])
        for r in range(4):
            nc.gpsimd.dma_start(
                out=w4sc_sb[r:P:32, :, :].bitcast(I32),
                in_=w4_scales[:, r:16:4, :].rearrange("a q c -> q a c").bitcast(I32),
            )
        nc.gpsimd.dma_start(out=gain_sb[:], in_=gain.rearrange("(p t) -> p t", t=PACK))

        def load_words(tile, words, t0, t1):
            nc.sync.dma_start(
                out=tile[:, t0:t1], in_=words[:, t0:t1, :].rearrange("p t i -> p (t i)").bitcast(I32)
            )

        pieces = [(half, a) for half in range(2) for a in range(PASSES)]
        w1_raw = held([P, len(pieces), PACK, HALF], F32, "w1_raw")

        nc.sync.dma_start(offs_sb[:], offs)
        load_words(tab_sb[0], tab_words[0], 0, T // 2)
        nc.sync.dma_start(
            out=tabsc_sb[0:P:4, :].bitcast(I32),
            in_=tab_scales[0:2].rearrange("a q t -> (a q) t").bitcast(I32),
        )
        nc.sync.dma_start(out=tabsc_sb[1:P:8, :].bitcast(I32), in_=tab_scales[2].bitcast(I32))
        load_words(tab_sb[0], tab_words[0], T // 2, T)
        nc.sync.dma_start(
            out=w4_sb[:].bitcast(I32), in_=w4_words.rearrange("a p c -> p a c").bitcast(I32)
        )
        nc.sync.dma_start(offs2_sb[:], offs2)
        for r in range(4):
            nc.sync.dma_start(
                out=tab2sc_sb[TAB2_ROW + r : P : 32, :].bitcast(I32),
                in_=tab2_scales[0, r:16:4, :].bitcast(I32),
            )

        warm = held([P, 1], F32, "warm")
        nc.scalar.activation(out=warm[:], in_=ident[:, 0:1], func=ACT.Ln, bias=1.0)

        wm_ps = bank(7)
        nc.tensor.transpose(wm_ps[:, 0:P], wm_rows[:], ident[:])
        wm_sb = held([P, MT], F32, "wm_sb")
        nc.scalar.copy(out=wm_sb[:], in_=wm_ps[:, 0:MT])

        v_sc = held([P, S], U8, "v_sc")
        nc.vector.tensor_copy(out=v_sc[:], in_=tabsc_sb[:].indirect(offs_sb[:]))

        def place_scale_rows(a):
            for r in range(4):
                rows = slice(64 * a + 4 * r, 64 * a + 64, 16) if a < 2 else slice(8 * r + 1, P, 32)
                nc.sync.dma_start(
                    out=v_planes[r:P:32, a, :].bitcast(I32), in_=v_sc[rows, :].bitcast(I32)
                )

        load_words(tab_sb[1], tab_words[1], 0, T // 2)
        place_scale_rows(0)
        load_words(tab_sb[1], tab_words[1], T // 2, T)
        place_scale_rows(1)
        load_words(tab_sb[2], tab_words[2], 0, T // 2)
        place_scale_rows(2)
        load_words(tab_sb[2], tab_words[2], T // 2, T)
        for i, (half, a) in enumerate(pieces):
            rows = w1[a * K_PASS : (a + 1) * K_PASS, half * HALF : (half + 1) * HALF]
            nc.sync.dma_start(out=w1_raw[:, i], in_=rows.rearrange("(p i) c -> p i c", i=PACK))
        load_words(tab2_sb, tab2_words[0], 0, T3)
        nc.sync.dma_start(pos2_sb[:], pos2)
        nc.sync.dma_start(pos1_sb[:], pos1)

        def gather_words(dst, table, offsets, j0, j1):
            nc.vector.tensor_copy(
                out=dst[:, j0:j1],
                in_=table[:].bitcast(U32).indirect(offsets[:, j0 // LANES : j1 // LANES]),
            )

        v_words = [held([P, S], U32, "v_words%d" % a) for a in range(PASSES)]

        def jcols(jt):
            return slice(jt * P, (jt + 1) * P)

        def trend_pass(acc, jt, a):
            nc.tensor.matmul_mx(
                out=acc[:],
                lhsT=v_words[a][:, jcols(jt)].bitcast(FP8X4),
                lhsT_scale=v_planes[:, a, jcols(jt)],
                rhs=w4_sb[:, a, :].bitcast(FP4X4),
                rhs_scale=w4sc_sb[:, a, :],
                start=(a == 0),
                stop=(a == PASSES - 1),
            )

        trend_ps = [bank(jt) for jt in range(JT)]
        for a in range(PASSES - 1):
            for jt in range(JT):
                if jt % 2 == 0:
                    gather_words(v_words[a], tab_sb[a], offs_sb, jt * P, (jt + 2) * P)
                trend_pass(trend_ps[jt], jt, a)

        v2_sc = held([P, S2], U8, "v2_sc")
        nc.vector.tensor_copy(out=v2_sc[:], in_=tab2sc_sb[:].indirect(offs2_sb[:]))

        neg_trend = [held([P, PACK, P], F32, "neg_trend%d" % jt) for jt in range(JT)]
        for jt in range(JT):
            if jt % 2 == 0:
                gather_words(v_words[2], tab_sb[2], offs_sb, jt * P, (jt + 2) * P)
            trend_pass(trend_ps[jt], jt, 2)
            nc.scalar.activation(
                out=neg_trend[jt][:],
                in_=trend_ps[jt][:].rearrange("p (q t) -> p t q", t=PACK),
                func=ACT.Copy,
                scale=-1.0,
            )

        w1_bf = held([P, PASSES * H * PACK], BF16, "w1_bf")
        w1_q = held([P, PASSES * H], U32, "w1_q")
        w1_sc = held([P, PASSES * H], U8, "w1_sc")

        def w1_quantise(i0, i1):
            cols = slice(i0 * HALF, i1 * HALF)
            rounded = w1_bf[:, i0 * HALF * PACK : i1 * HALF * PACK]
            nc.vector.tensor_copy(
                out=rounded.rearrange("p (a c n i) -> p a c i n", a=i1 - i0, n=4, i=PACK),
                in_=w1_raw[:, i0:i1].rearrange("p a i (c n) -> p a c i n", n=4),
            )
            nc.vector.quantize_mx(out=w1_q[:, cols].bitcast(FP8X4), scales=w1_sc[:, cols], in_=rounded)

        ring_ps = [[bank(half * 4 + pair) for pair in range(JT // 2)] for half in range(2)]
        for i, (half, a) in enumerate(pieces):
            if a == 0:
                w1_quantise(i, i + 2)
            if a == 2:
                w1_quantise(i, i + 1)
            cols = slice(i * HALF, (i + 1) * HALF)
            for jt in range(JT):
                nc.tensor.matmul_mx(
                    out=ring_ps[half][jt // 2][:, (jt % 2) * HALF : (jt % 2 + 1) * HALF],
                    lhsT=v_words[a][:, jcols(jt)].bitcast(FP8X4),
                    lhsT_scale=v_planes[:, a, jcols(jt)],
                    rhs=w1_q[:, cols].bitcast(FP8X4),
                    rhs_scale=w1_sc[:, cols],
                    start=(a == 0 and jt % 2 == 0),
                    stop=(a == PASSES - 1 and jt % 2 == 1),
                )

        def add_transposed(acc, src, first):
            for t in range(PACK):
                nc.tensor.matmul(
                    acc[:, t * P : (t + 1) * P],
                    lhsT=src[:, t, :],
                    rhs=ident[:],
                    is_transpose=True,
                    start=(first and t == 0),
                    stop=(not first and t == PACK - 1),
                )

        h_bf = held([P, (S - P) * PACK], BF16, "h_bf")
        h_bf_last = held([P, P * PACK], BF16, "h_bf_last")
        h_q = held([P, S], U32, "h_q")
        h_sc = held([P, S], U8, "h_sc")
        v2_words = []

        def gather_stocks(i, name):
            v2_words.append(held([P, 2 * P], U32, name))
            nc.vector.tensor_copy(
                out=v2_words[i][:],
                in_=tab2_sb[:].bitcast(U32).indirect(offs2_sb[:, 2 * i * P // LANES : 2 * (i + 1) * P // LANES]),
            )

        logs = [held([P, 2, PACK, P], F32, "logs%d" % pair) for pair in range(JT // 2)]
        quantise_after = {3: 0, 6: 4, 7: 7}

        def magnitudes(half, pair, u0, u1):
            mag = work.tile([P, u1 - u0, PACK, P // 2], F32, name="mag")
            ring = ring_ps[half][pair][:].rearrange("p (u q t) -> p u t q", u=2, t=PACK)
            nc.scalar.activation(out=mag[:], in_=ring[:, u0:u1], func=ACT.Abs)
            return mag

        def logarithms(half, pair, u0, u1, mag):
            rows = slice(half * P // 2, (half + 1) * P // 2)
            nc.scalar.activation(out=logs[pair][:, u0:u1, :, rows], in_=mag[:], func=ACT.Ln, bias=1.0)

        diff_ps = {}

        def open_difference(jt):
            diff_ps[jt] = bank(jt)
            add_transposed(diff_ps[jt], neg_trend[jt], True)

        def finish_features(jt):
            add_transposed(diff_ps[jt], logs[jt // 2][:, jt % 2], False)
            rounded = h_bf_last[:] if jt == JT - 1 else h_bf[:, jt * K_PASS : (jt + 1) * K_PASS]
            nc.vector.tensor_tensor(
                out=rounded.rearrange("p (n t) -> p n t", t=PACK),
                in0=diff_ps[jt][:].rearrange("p (t n) -> p n t", t=PACK),
                in1=gain_sb[:].unsqueeze(1).to_broadcast([P, P, PACK]),
                op=ALU.mult,
            )
            if jt in quantise_after:
                j0, j1 = quantise_after[jt] * P, (jt + 1) * P
                nc.vector.quantize_mx(
                    out=h_q[:, j0:j1].bitcast(FP8X4),
                    scales=h_sc[:, j0:j1],
                    in_=rounded if jt == JT - 1 else h_bf[:, j0 * PACK : j1 * PACK],
                )

        for pair in range(JT // 2):
            mag = magnitudes(0, pair, 0, 2)
            open_difference(pair)
            logarithms(0, pair, 0, 2, mag)
        for i in range(3):
            gather_stocks(i, "v2_words%d" % i)
        last = JT // 2 - 1
        for pair in range(last):
            mag = magnitudes(1, pair, 0, 2)
            logarithms(1, pair, 0, 2, mag)
            finish_features(2 * pair)
            open_difference(JT // 2 + pair)
            finish_features(2 * pair + 1)
        mag = magnitudes(1, last, 0, 1)
        logarithms(1, last, 0, 1, mag)
        mag = magnitudes(1, last, 1, 2)
        open_difference(JT - 1)
        finish_features(JT - 2)
        logarithms(1, last, 1, 2, mag)
        finish_features(JT - 1)
        gather_stocks(3, "h_bf_last")

        score_banks = [(0, 1), (2, 3), (4, 5), (6, 7)]
        margins = {}
        weighted = {}
        sums = {}
        scores = {}

        def score_pass(acc, m, base, c0, c1):
            nc.tensor.matmul_mx(
                out=acc[:, c0:c1],
                lhsT=v2_words[m // 2][:, jcols(m % 2)].bitcast(FP8X4),
                lhsT_scale=v2_sc[TAB2_ROW:P, jcols(m)],
                rhs=h_q[:, base + c0 : base + c1].bitcast(FP8X4),
                rhs_scale=h_sc[:, base + c0 : base + c1],
                start=True,
                stop=True,
            )

        def make_scores(m):
            scores[m] = work.tile([P, S], F32, name="scores", bufs=4)
            for half in range(2):
                cols = slice(half * BANK, (half + 1) * BANK)
                acc = bank(score_banks[m % 4][half])
                if m == 0 and half == 1:
                    score_pass(acc, m, BANK, 0, 2 * P)
                    score_pass(acc, m, BANK, 2 * P, 3 * P)
                    nc.scalar.copy(out=scores[m][:, BANK : BANK + 3 * P], in_=acc[:, 0 : 3 * P])
                    score_pass(acc, m, BANK, 3 * P, BANK)
                    nc.scalar.copy(out=scores[m][:, BANK + 3 * P : S], in_=acc[:, 3 * P : BANK])
                else:
                    score_pass(acc, m, half * BANK, 0, BANK)
                    nc.scalar.copy(out=scores[m][:, cols], in_=acc[:])
            margins[m] = work.tile([P, PAIRS], F32, name="margin")
            nc.vector.tensor_copy(out=margins[m][:], in_=scores[m][:].indirect(pos2_sb[:]))

        def weigh(m):
            weighted[m] = work.tile([P, PAIRS], F32, name="weighted")
            nc.scalar.activation(
                out=weighted[m][:], in_=margins[m][:], func=ACT.Copy, scale=wm_sb[:, m : m + 1]
            )

        def parts(m):
            if m < MT - 1:
                return [(0, PAIRS)]
            return [(0, 2 * P), (2 * P, 3 * P), (3 * P, PAIRS)]

        def add_cores(m):
            sums[m] = work.tile([P, PAIRS], F32, name="sums", bufs=4)
            for c0, c1 in parts(m):
                nc.vector.tensor_tensor(
                    out=sums[m][:, c0:c1],
                    in0=scores[m][:].indirect(pos1_sb[:, c0 // LANES : c1 // LANES]),
                    in1=weighted[m][:, c0:c1],
                    op=ALU.add,
                )

        def finish(m):
            result = work.tile([P, PAIRS], F32, name="result")
            for c0, c1 in parts(m):
                nc.scalar.activation(out=result[:, c0:c1], in_=sums[m][:, c0:c1], func=ACT.Silu)
                nc.sync.dma_start(out=out[m * P : (m + 1) * P, c0:c1], in_=result[:, c0:c1])

        for step in range(MT + 3):
            if step < MT:
                make_scores(step)
            if 1 <= step <= MT:
                weigh(step - 1)
                add_cores(step - 1)
            if step >= 3:
                finish(step - 3)
